import numpy as np
import ml_dtypes


def mxq(x, axis, fmt="e4m3"):
    dtype, down = {"e4m3": (ml_dtypes.float8_e4m3fn, 7), "e5m2": (ml_dtypes.float8_e5m2, 14)}[fmt]
    v = np.moveaxis(np.asarray(x, np.float32).astype(ml_dtypes.bfloat16).astype(np.float64), axis, -1)
    blocks = v.reshape(v.shape[:-1] + (-1, 32))
    amax = np.abs(blocks).max(-1, keepdims=True)
    byte = np.maximum(np.where(amax > 0, np.frexp(amax)[1] - 1 + 127, 0) - down, 1)
    scale = np.exp2(byte - 127.0)
    codes = (blocks / scale).astype(np.float32).astype(dtype).astype(np.float64)
    return np.moveaxis((codes * scale).reshape(v.shape), -1, axis)


WIDE = False


def mx_kscale(k):
    if not WIDE:
        return np.ones(k)
    levels = np.array([10, -10, 5, -5, 0])
    if k % 512:
        return np.exp2(np.random.permutation(np.resize(levels, k // 32))).repeat(32)
    a = np.empty((k // 512, 16))
    for p in range(k // 512):
        a[p, :8] = np.random.permutation(np.resize(levels, 8))
        for g in range(8):
            far = levels[np.abs(levels - a[p, g]) >= 10]
            a[p, g + 8] = far[np.random.randint(len(far))]
    return np.exp2(a.ravel()).repeat(32)


def f64(x):
    return np.asarray(x).astype(np.float64)


def striped(idx):
    return np.tile(np.asarray(idx).reshape(-1, 16).T, (8, 1)).astype(np.uint16)


def unstriped(offs):
    return offs[:16].T.reshape(-1).astype(np.int64)


E2M1 = np.array([0.0, 0.5, 1.0, 1.5, 2.0, 3.0, 4.0, 6.0, -0.0, -0.5, -1.0, -1.5, -2.0, -3.0, -4.0, -6.0])


def pack_weight(w, fmt):
    k, n = w.shape
    w = f64(np.asarray(w, np.float32).astype(ml_dtypes.bfloat16)).reshape(k // 32, 32, n)
    amax = np.abs(w).max(1)
    if fmt == "e4m3":
        byte = np.frexp(amax)[1] - 1 + 127 - 7
    else:
        mant, ex = np.frexp(amax / 6.0)
        byte = np.where(mant > 0.5, ex, ex - 1) + 127
    byte = np.clip(np.where(amax > 0, byte, 1), 1, 254)
    scaled = (w * np.exp2(127.0 - byte)[:, None, :]).reshape(k, n).astype(np.float32)
    by_word = np.ascontiguousarray(scaled.reshape(k // 512, 128, 4, n).transpose(0, 1, 3, 2))
    if fmt == "e4m3":
        words = by_word.astype(ml_dtypes.float8_e4m3fn).view(np.uint8)
    else:
        c = by_word.astype(ml_dtypes.float4_e2m1fn).view(np.uint8) & 0xF
        words = (c[..., 0::2] | (c[..., 1::2] << 4)).reshape(k // 512, 128, 2 * n)
    return np.ascontiguousarray(words), np.ascontiguousarray(byte.astype(np.uint8).reshape(k // 512, 16, n))


def unpack_weight(words, scales, fmt):
    g, _, n = scales.shape
    words = np.ascontiguousarray(words).reshape(g, 128, n, -1)
    if fmt == "e4m3":
        vals = words.view(ml_dtypes.float8_e4m3fn).astype(np.float64)
    else:
        nib = np.empty((g, 128, n, 4), np.uint8)
        nib[..., 0::2] = words & 0xF
        nib[..., 1::2] = words >> 4
        vals = E2M1[nib]
    vals = vals * np.repeat(np.exp2(scales.astype(np.float64) - 127.0), 8, axis=1)[..., None]
    return vals.transpose(0, 1, 3, 2).reshape(g * 512, n)


D, E, T, I, Q, G = 512, 512, 2048, 512, 128, 64


def setup_inputs():
    n = np.random.standard_normal
    idx = np.random.permutation(T)[:I]
    fd = mx_kscale(D)
    fe = mx_kscale(E)
    keysp = pack_weight(n((D, T)) / fd[:, None], "e2m1")
    valsp = pack_weight(n((E, T)) / fe[:, None], "e2m1")
    return {
        "query": (n((D, Q)) * 0.8 / np.sqrt(D) * fd[:, None]).astype(np.float32),
        "query2": (n((D, Q)) * 0.8 / np.sqrt(D) * fd[:, None]).astype(np.float32),
        "keys_words": keysp[0],
        "keys_scales": keysp[1],
        "gout": (n((E, Q)) * 1 / np.sqrt(E) * fe[:, None]).astype(np.float32),
        "vals_words": valsp[0],
        "vals_scales": valsp[1],
        "old": (0.5 * n((Q, T))).astype(np.float32),
        "offs": striped(idx),
    }


def reference(query, query2, keys_words, keys_scales, gout, vals_words, vals_scales, old, offs):
    idx = unstriped(offs)
    keysu = unpack_weight(keys_words, keys_scales, "e2m1")
    valsu = unpack_weight(vals_words, vals_scales, "e2m1")
    queryq = mxq(f64(query), 0, "e4m3")
    keysidxg = keysu[:, idx]
    a = queryq.T @ keysidxg
    query2q = mxq(f64(query2), 0, "e4m3")
    b = query2q.T @ keysidxg
    pa = np.exp(a)
    sa = pa.reshape(Q, G, I // G).sum(axis=2)
    z = np.sum(sa, axis=1, keepdims=True)
    pb = np.exp(b)
    sb = pb.reshape(Q, G, I // G).sum(axis=2)
    goutq = mxq(f64(gout), 0, "e4m3")
    valsidxg = valsu[:, idx]
    c0 = goutq.T @ valsidxg
    drr = c0 * pb
    dr = drr.reshape(Q, G, I // G).sum(axis=2)
    dz = np.sum(dr / sb * sa / np.square(z) * (-1.0), axis=1, keepdims=True)
    dsa = dr / sb / z + dz
    r1 = np.repeat(dsa, I // G, axis=1)
    da = r1 * pa
    gs = da * 512.0
    gf = np.zeros((Q, T))
    gf[:, idx] = gs
    y = f64(old) + gf
    return y

@@ -1,0 +1,179 @@
+from contextlib import ExitStack
+
+import concourse.mybir as mybir
+
+D, T, I, Q, G = 512, 2048, 512, 128, 64
+PAGE = I // G
+P = 128
+PACK = 4
+GAIN = 512.0
+FLOPS = 3 * 2 * D * Q * I
+
+F32 = mybir.dt.float32
+BF16 = mybir.dt.bfloat16
+I32 = mybir.dt.int32
+U32 = mybir.dt.uint32
+U16 = mybir.dt.uint16
+U8 = mybir.dt.uint8
+FP8X4 = mybir.dt.float8_e4m3fn_x4
+FP4X4 = mybir.dt.float4_e2m1fn_x4
+ALU = mybir.AluOpType
+ACT = mybir.ActivationFunctionType
+AX = mybir.AxisListType
+
+STORE_COLS = (512, 512, 512, 256, 256)
+
+
+def tile_attend_bpagethensecond_s_kernel(
+    tc, query, query2, keys_words, keys_scales, gout, vals_words, vals_scales, old, offs, out
+):
+    nc = tc.nc
+    with ExitStack() as ctx:
+        held = ctx.enter_context(tc.tile_pool(name="held", bufs=1))
+        psum = ctx.enter_context(tc.psum_pool(name="psum", bufs=1))
+
+        offsets = held.tile([P, I // 16], U16, name="offsets")
+        nc.sync.dma_start(offsets[:], offs)
+
+        def load_words(words, queue):
+            tile = held.tile([P, T], U16, name="pool_words", tag="pool_words", align_bytes=64)
+            queue.dma_start(tile[:].bitcast(I32), words[0].bitcast(I32))
+            return tile
+
+        def load_scales(scales, name):
+            tile = held.tile([P, T], U8, name=name, tag=name, align_bytes=64)
+            nc.vector.memset(tile[:].bitcast(I32), 0)
+            for quad in range(4):
+                nc.sync.dma_start(
+                    tile[32 * quad : 32 * quad + 4, :].bitcast(I32),
+                    scales[0, 4 * quad : 4 * quad + 4, :].bitcast(I32),
+                )
+            return tile
+
+        def load_rows(x, tag, queue):
+            raw = held.tile([P, PACK, Q], F32, name=tag, tag=tag)
+            queue.dma_start(raw[:], x.rearrange("(p j) w -> p j w", j=PACK))
+            return raw
+
+        def interleave(raw, name):
+            grouped = held.tile([P, Q, PACK], BF16, name=name, align_bytes=64)
+            nc.scalar.copy(grouped[:], raw[:].rearrange("p j w -> p w j"))
+            return grouped
+
+        def quantize(grouped, name):
+            codes = held.tile([P, Q], U32, name=name + "_codes", align_bytes=64)
+            plane = held.tile([P, Q], U8, name=name + "_plane", align_bytes=64)
+            nc.vector.quantize_mx(
+                out=codes[:].bitcast(FP8X4),
+                scales=plane[:],
+                in_=grouped[:].rearrange("p w j -> p (w j)"),
+            )
+            return codes, plane
+
+        def gather(table, dtype, name):
+            picked = held.tile([P, I], dtype, name=name, align_bytes=64)
+            nc.vector.tensor_copy(picked[:], table[:].indirect(offsets[:]))
+            return picked
+
+        def scores(quantized, words, plane, name):
+            acc = psum.tile([P, I], F32, name=name)
+            nc.tensor.matmul_mx(
+                out=acc[:],
+                lhsT=quantized[0][:].bitcast(FP8X4),
+                lhsT_scale=quantized[1][:],
+                rhs=words[:].bitcast(FP4X4),
+                rhs_scale=plane[:],
+                start=True,
+                stop=True,
+            )
+            return acc
+
+        def by_page(ap):
+            return ap.rearrange("p (g j) -> p g j", j=PAGE)
+
+        def over_page(ap):
+            return ap.unsqueeze(2).to_broadcast([P, G, PAGE])
+
+        key_words = load_words(keys_words, nc.sync)
+        key_scales = load_scales(keys_scales, "key_scales")
+        raw_q2 = load_rows(query2, "raw_second", nc.sync)
+        raw_q = load_rows(query, "raw_first", nc.sync)
+        val_scales = load_scales(vals_scales, "val_scales")
+        window = held.tile([P, T], F32, name="window")
+        nc.vector.memset(window[:], 0.0)
+
+        warm = held.tile([P, 1], F32, name="warm")
+        nc.scalar.activation(warm[:], window[:, 0:1], ACT.Exp)
+
+        key_codes = gather(key_words, U16, "key_codes")
+        key_plane = gather(key_scales, U8, "key_plane")
+        grouped_q2 = interleave(raw_q2, "grouped_q2")
+        grouped_q = interleave(raw_q, "grouped_q")
+        q2 = quantize(grouped_q2, "q2")
+        b = scores(q2, key_codes, key_plane, "b")
+        q1 = quantize(grouped_q, "q1")
+        a = scores(q1, key_codes, key_plane, "a")
+
+        raw_g = load_rows(gout, "raw_second", nc.sync)
+        val_words = load_words(vals_words, nc.sync)
+        grouped_g = interleave(raw_g, "grouped_g")
+
+        val_plane = gather(val_scales, U8, "val_plane")
+
+        page_max = held.tile([P, G], F32, name="page_max")
+        nc.vector.tensor_reduce(page_max[:], by_page(b[:]), AX.X, ALU.max)
+        neg_row_max = held.tile([P, 1], F32, name="neg_row_max")
+        nc.vector.tensor_reduce(neg_row_max[:], a[:], AX.X, ALU.max, negate=True)
+        shifted = held.tile([P, I], F32, name="shifted")
+        nc.vector.tensor_tensor(by_page(shifted[:]), by_page(b[:]), over_page(page_max[:]), ALU.subtract)
+
+        weights = held.tile([P, 2, I], F32, name="weights")
+        pa, pb = weights[:, 0, :], weights[:, 1, :]
+        z = held.tile([P, 1], F32, name="z")
+        nc.scalar.activation(pa, a[:], ACT.Exp, bias=neg_row_max[:], accum_out=z[:])
+        nc.scalar.activation(pb, shifted[:], ACT.Exp)
+
+        val_codes = gather(val_words, U16, "val_codes")
+        g = quantize(grouped_g, "g")
+        c = scores(g, val_codes, val_plane, "c")
+
+        before = []
+        for half in range(2):
+            part = held.tile([P, T // 2], F32, name="before%d" % half, tag="pool_words" if half == 0 else "val_scales", align_bytes=64)
+            nc.sync.dma_start(part[:], old[:, half * (T // 2) : (half + 1) * (T // 2)])
+            before.append(part)
+
+        sums = held.tile([P, 2 * G], F32, name="sums")
+        nc.vector.tensor_reduce(sums[:], weights[:].rearrange("p s (g j) -> p (s g) j", j=PAGE), AX.X, ALU.add)
+        sa, sb = sums[:, :G], sums[:, G:]
+        inv_z = held.tile([P, 1], F32, name="inv_z")
+        nc.vector.reciprocal(inv_z[:], z[:])
+
+        drr = held.tile([P, I], F32, name="drr")
+        nc.vector.tensor_tensor(drr[:], c[:], pb, ALU.mult)
+        inv_sb = held.tile([P, G], F32, name="inv_sb")
+        nc.vector.reciprocal(inv_sb[:], sb)
+        dr = held.tile([P, G], F32, name="dr")
+        nc.vector.tensor_reduce(dr[:], by_page(drr[:]), AX.X, ALU.add)
+        share = held.tile([P, G], F32, name="share")
+        nc.vector.scalar_tensor_tensor(share[:], sa, inv_z[:], inv_sb[:], ALU.mult, ALU.mult)
+
+        page_grad = held.tile([P, G], F32, name="page_grad")
+        nc.vector.scalar_tensor_tensor(page_grad[:], dr[:], GAIN, inv_sb[:], ALU.mult, ALU.mult)
+        weighted = held.tile([P, G], F32, name="weighted")
+        mean_grad = held.tile([P, 1], F32, name="mean_grad")
+        nc.vector.scalar_tensor_tensor(weighted[:], dr[:], GAIN, share[:], ALU.mult, ALU.mult, accum_out=mean_grad[:])
+
+        r1 = held.tile([P, I], F32, name="r1")
+        nc.vector.tensor_scalar(by_page(r1[:]), over_page(page_grad[:]), mean_grad[:], inv_z[:], ALU.subtract, ALU.mult)
+        pa_whole = pa
+        nc.vector.tensor_tensor(window[:].indirect(offsets[:]), r1[:], pa_whole, ALU.mult)
+
+        start = 0
+        for n, width in enumerate(STORE_COLS):
+            result = held.tile([P, width], F32, name="result%d" % n)
+            half, at = divmod(start, T // 2)
+            nc.vector.tensor_tensor(result[:], window[:, start : start + width], before[half][:, at : at + width], ALU.add)
+            queue = nc.sync if n % 2 == 0 else nc.scalar
+            queue.dma_start(out[:, start : start + width], result[:])
+            start = start + width

@@ -1,6 +1,9 @@
 from contextlib import ExitStack
 
+import math
+
 import concourse.mybir as mybir
+from concourse.masks import make_identity
 
 D, T, I, Q, G = 512, 2048, 512, 128, 64
 PAGE = I // G
@@ -21,7 +24,10 @@ ALU = mybir.AluOpType
 ACT = mybir.ActivationFunctionType
 AX = mybir.AxisListType
 
-STORE_COLS = (512, 512, 512, 256, 256)
+STORE_COLS = (256, 256, 512, 512, 256, 256)
+SOFTEN = 8.0
+QUARTER = 4
+HALF = I // 2
 
 
 def tile_attend_bpagethensecond_s_kernel(
@@ -35,9 +41,9 @@ def tile_attend_bpagethensecond_s_kernel(
         offsets = held.tile([P, I // 16], U16, name="offsets")
         nc.sync.dma_start(offsets[:], offs)
 
-        def load_words(words, queue):
-            tile = held.tile([P, T], U16, name="pool_words", tag="pool_words", align_bytes=64)
-            queue.dma_start(tile[:].bitcast(I32), words[0].bitcast(I32))
+        def load_words(words, name):
+            tile = held.tile([P, T], U16, name=name, align_bytes=64)
+            nc.sync.dma_start(tile[:].bitcast(I32), words[0].bitcast(I32))
             return tile
 
         def load_scales(scales, name):
@@ -51,17 +57,17 @@ def tile_attend_bpagethensecond_s_kernel(
             return tile
 
         def load_rows(x, tag, queue):
-            raw = held.tile([P, PACK, Q], F32, name=tag, tag=tag)
+            raw = held.tile([P, PACK, Q], F32, name=tag, tag=tag, align_bytes=64)
             queue.dma_start(raw[:], x.rearrange("(p j) w -> p j w", j=PACK))
             return raw
 
         def interleave(raw, name):
-            grouped = held.tile([P, Q, PACK], BF16, name=name, align_bytes=64)
-            nc.scalar.copy(grouped[:], raw[:].rearrange("p j w -> p w j"))
+            grouped = held.tile([P, Q, PACK], BF16, name=name, tag=name, align_bytes=64)
+            nc.scalar.activation(grouped[:], raw[:].rearrange("p j w -> p w j"), ACT.Copy)
             return grouped
 
         def quantize(grouped, name):
-            codes = held.tile([P, Q], U32, name=name + "_codes", align_bytes=64)
+            codes = held.tile([P, Q], U32, name=name + "_codes", tag=name, align_bytes=64)
             plane = held.tile([P, Q], U8, name=name + "_plane", align_bytes=64)
             nc.vector.quantize_mx(
                 out=codes[:].bitcast(FP8X4),
@@ -75,17 +81,19 @@ def tile_attend_bpagethensecond_s_kernel(
             nc.vector.tensor_copy(picked[:], table[:].indirect(offsets[:]))
             return picked
 
-        def scores(quantized, words, plane, name):
+        def scores(quantized, words, plane, name, width=I):
             acc = psum.tile([P, I], F32, name=name)
-            nc.tensor.matmul_mx(
-                out=acc[:],
-                lhsT=quantized[0][:].bitcast(FP8X4),
-                lhsT_scale=quantized[1][:],
-                rhs=words[:].bitcast(FP4X4),
-                rhs_scale=plane[:],
-                start=True,
-                stop=True,
-            )
+            for first in range(0, I, width):
+                slots = slice(first, first + width)
+                nc.tensor.matmul_mx(
+                    out=acc[:, slots],
+                    lhsT=quantized[0][:].bitcast(FP8X4),
+                    lhsT_scale=quantized[1][:],
+                    rhs=words[:, slots].bitcast(FP4X4),
+                    rhs_scale=plane[:, slots],
+                    start=True,
+                    stop=True,
+                )
             return acc
 
         def by_page(ap):
@@ -94,86 +102,107 @@ def tile_attend_bpagethensecond_s_kernel(
         def over_page(ap):
             return ap.unsqueeze(2).to_broadcast([P, G, PAGE])
 
-        key_words = load_words(keys_words, nc.sync)
+        key_words = load_words(keys_words, "key_words")
         key_scales = load_scales(keys_scales, "key_scales")
-        raw_q2 = load_rows(query2, "raw_second", nc.sync)
         raw_q = load_rows(query, "raw_first", nc.sync)
+        raw_q2 = load_rows(query2, "raw_second", nc.sync)
+        val_words = load_words(vals_words, "val_words")
+        raw_g = load_rows(gout, "raw_grad", nc.sync)
         val_scales = load_scales(vals_scales, "val_scales")
+        identity = held.tile([P, P], F32, name="identity")
+        make_identity(nc, identity[:])
         window = held.tile([P, T], F32, name="window")
         nc.vector.memset(window[:], 0.0)
 
-        warm = held.tile([P, 1], F32, name="warm")
-        nc.scalar.activation(warm[:], window[:, 0:1], ACT.Exp)
-
         key_codes = gather(key_words, U16, "key_codes")
         key_plane = gather(key_scales, U8, "key_plane")
-        grouped_q2 = interleave(raw_q2, "grouped_q2")
         grouped_q = interleave(raw_q, "grouped_q")
-        q2 = quantize(grouped_q2, "q2")
-        b = scores(q2, key_codes, key_plane, "b")
+        grouped_q2 = interleave(raw_q2, "grouped_q2")
         q1 = quantize(grouped_q, "q1")
         a = scores(q1, key_codes, key_plane, "a")
+        q2 = quantize(grouped_q2, "q2")
+        b = scores(q2, key_codes, key_plane, "b")
 
-        raw_g = load_rows(gout, "raw_second", nc.sync)
-        val_words = load_words(vals_words, nc.sync)
         grouped_g = interleave(raw_g, "grouped_g")
 
-        val_plane = gather(val_scales, U8, "val_plane")
+        before = held.tile([P, T], F32, name="before", tag="raw_grad", align_bytes=64)
+        nc.sync.dma_start(before[:], old)
+        val_codes = held.tile([P, I], U16, name="val_codes", tag="raw_second", align_bytes=64)
+        nc.vector.tensor_copy(val_codes[:], val_words[:].indirect(offsets[:]))
 
         page_max = held.tile([P, G], F32, name="page_max")
         nc.vector.tensor_reduce(page_max[:], by_page(b[:]), AX.X, ALU.max)
-        neg_row_max = held.tile([P, 1], F32, name="neg_row_max")
-        nc.vector.tensor_reduce(neg_row_max[:], a[:], AX.X, ALU.max, negate=True)
-        shifted = held.tile([P, I], F32, name="shifted")
+        pa = held.tile([P, I], F32, name="pa")
+        soft_sum = held.tile([P, 1], F32, name="soft_sum", tag="val_plane", align_bytes=64)
+        nc.scalar.activation(pa[:], a[:], ACT.Exp, scale=1.0 / SOFTEN, accum_out=soft_sum[:])
+        neg_shift = held.tile([P, 1], F32, name="neg_shift")
+        nc.vector.tensor_scalar(
+            neg_shift[:], soft_sum[:].bitcast(I32), -SOFTEN * math.log(2.0) / 2**23, SOFTEN * math.log(2.0) * 127, ALU.mult, ALU.add
+        )
+        g = quantize(grouped_g, "g")
+        shifted = held.tile([P, I], F32, name="shifted", tag="shifted")
         nc.vector.tensor_tensor(by_page(shifted[:]), by_page(b[:]), over_page(page_max[:]), ALU.subtract)
 
-        weights = held.tile([P, 2, I], F32, name="weights")
-        pa, pb = weights[:, 0, :], weights[:, 1, :]
         z = held.tile([P, 1], F32, name="z")
-        nc.scalar.activation(pa, a[:], ACT.Exp, bias=neg_row_max[:], accum_out=z[:])
-        nc.scalar.activation(pb, shifted[:], ACT.Exp)
+        nc.scalar.activation(pa[:], a[:], ACT.Exp, bias=neg_shift[:], accum_out=z[:])
+        pb = held.tile([P, I], F32, name="pb")
+        nc.scalar.activation(pb[:], shifted[:], ACT.Exp)
 
-        val_codes = gather(val_words, U16, "val_codes")
-        g = quantize(grouped_g, "g")
-        c = scores(g, val_codes, val_plane, "c")
-
-        before = []
+        val_plane = held.tile([P, I], U8, name="val_plane", tag="val_plane", align_bytes=64)
         for half in range(2):
-            part = held.tile([P, T // 2], F32, name="before%d" % half, tag="pool_words" if half == 0 else "val_scales", align_bytes=64)
-            nc.sync.dma_start(part[:], old[:, half * (T // 2) : (half + 1) * (T // 2)])
-            before.append(part)
+            nc.vector.tensor_copy(
+                val_plane[:, half * HALF : (half + 1) * HALF],
+                val_scales[:].indirect(offsets[:, half * HALF // 16 : (half + 1) * HALF // 16]),
+            )
 
-        sums = held.tile([P, 2 * G], F32, name="sums")
-        nc.vector.tensor_reduce(sums[:], weights[:].rearrange("p s (g j) -> p (s g) j", j=PAGE), AX.X, ALU.add)
-        sa, sb = sums[:, :G], sums[:, G:]
+        turned = psum.tile([P, Q], F32, name="turned")
+        for j in range(QUARTER):
+            nc.tensor.matmul(
+                turned[:], pa[:, j::QUARTER], identity[:], start=(j == 0), stop=(j == QUARTER - 1), is_transpose=True
+            )
+        c = scores(g, val_codes, val_plane, "c", HALF)
+        turned_sb = held.tile([P, Q], F32, name="turned_sb")
+        nc.scalar.copy(turned_sb[:], turned[:])
+        half_sums = psum.tile([P, 2 * G], F32, name="half_sums")
+        nc.tensor.transpose(half_sums[:], turned_sb[:], identity[:])
+
+        sb = held.tile([P, G], F32, name="sb")
+        nc.vector.tensor_reduce(sb[:], by_page(pb[:]), AX.X, ALU.add)
         inv_z = held.tile([P, 1], F32, name="inv_z")
         nc.vector.reciprocal(inv_z[:], z[:])
 
         drr = held.tile([P, I], F32, name="drr")
-        nc.vector.tensor_tensor(drr[:], c[:], pb, ALU.mult)
-        inv_sb = held.tile([P, G], F32, name="inv_sb")
-        nc.vector.reciprocal(inv_sb[:], sb)
+        nc.vector.tensor_tensor(drr[:], c[:], pb[:], ALU.mult)
+        inv_sb = held.tile([P, G], F32, name="inv_sb", tag="val_plane", align_bytes=64)
+        nc.vector.reciprocal(inv_sb[:], sb[:])
         dr = held.tile([P, G], F32, name="dr")
         nc.vector.tensor_reduce(dr[:], by_page(drr[:]), AX.X, ALU.add)
-        share = held.tile([P, G], F32, name="share")
-        nc.vector.scalar_tensor_tensor(share[:], sa, inv_z[:], inv_sb[:], ALU.mult, ALU.mult)
+
+        def by_half(ap):
+            return ap.rearrange("p (g h) -> p g h", h=2)
+
+        def over_half(ap):
+            return ap.unsqueeze(2).to_broadcast([P, G, 2])
+
+        share = held.tile([P, 2 * G], F32, name="share")
+        nc.vector.scalar_tensor_tensor(by_half(share[:]), by_half(half_sums[:]), inv_z[:], over_half(inv_sb[:]), ALU.mult, ALU.mult)
 
         page_grad = held.tile([P, G], F32, name="page_grad")
         nc.vector.scalar_tensor_tensor(page_grad[:], dr[:], GAIN, inv_sb[:], ALU.mult, ALU.mult)
-        weighted = held.tile([P, G], F32, name="weighted")
+        weighted = held.tile([P, 2 * G], F32, name="weighted")
         mean_grad = held.tile([P, 1], F32, name="mean_grad")
-        nc.vector.scalar_tensor_tensor(weighted[:], dr[:], GAIN, share[:], ALU.mult, ALU.mult, accum_out=mean_grad[:])
+        nc.vector.scalar_tensor_tensor(
+            by_half(weighted[:]), over_half(dr[:]), GAIN, by_half(share[:]), ALU.mult, ALU.mult, accum_out=mean_grad[:]
+        )
 
         r1 = held.tile([P, I], F32, name="r1")
         nc.vector.tensor_scalar(by_page(r1[:]), over_page(page_grad[:]), mean_grad[:], inv_z[:], ALU.subtract, ALU.mult)
-        pa_whole = pa
-        nc.vector.tensor_tensor(window[:].indirect(offsets[:]), r1[:], pa_whole, ALU.mult)
+        nc.vector.tensor_tensor(window[:].indirect(offsets[:]), r1[:], pa[:], ALU.mult)
 
         start = 0
         for n, width in enumerate(STORE_COLS):
             result = held.tile([P, width], F32, name="result%d" % n)
-            half, at = divmod(start, T // 2)
-            nc.vector.tensor_tensor(result[:], window[:, start : start + width], before[half][:, at : at + width], ALU.add)
+            nc.vector.tensor_tensor(result[:], window[:, start : start + width], before[:, start : start + width], ALU.add)
             queue = nc.sync if n % 2 == 0 else nc.scalar
             queue.dma_start(out[:, start : start + width], result[:])
             start = start + width

@@ -39,7 +39,6 @@ def tile_attend_bpagethensecond_s_kernel(
         psum = ctx.enter_context(tc.psum_pool(name="psum", bufs=1))
 
         offsets = held.tile([P, I // 16], U16, name="offsets")
-        nc.sync.dma_start(offsets[:], offs)
 
         def load_words(words, name):
             tile = held.tile([P, T], U16, name=name, align_bytes=64)
@@ -103,16 +102,18 @@ def tile_attend_bpagethensecond_s_kernel(
             return ap.unsqueeze(2).to_broadcast([P, G, PAGE])
 
         key_words = load_words(keys_words, "key_words")
+        nc.sync.dma_start(offsets[:], offs)
         key_scales = load_scales(keys_scales, "key_scales")
         raw_q = load_rows(query, "raw_first", nc.sync)
         raw_q2 = load_rows(query2, "raw_second", nc.sync)
         val_words = load_words(vals_words, "val_words")
         raw_g = load_rows(gout, "raw_grad", nc.sync)
         val_scales = load_scales(vals_scales, "val_scales")
-        identity = held.tile([P, P], F32, name="identity")
-        make_identity(nc, identity[:])
         window = held.tile([P, T], F32, name="window")
         nc.vector.memset(window[:], 0.0)
+        identity = held.tile([P, P], F32, name="identity")
+        nc.vector.memset(identity[:], 0.0)
+        make_identity(nc, identity[:], nomemset=True)
 
         key_codes = gather(key_words, U16, "key_codes")
         key_plane = gather(key_scales, U8, "key_plane")
@@ -136,15 +137,20 @@ def tile_attend_bpagethensecond_s_kernel(
         soft_sum = held.tile([P, 1], F32, name="soft_sum", tag="val_plane", align_bytes=64)
         nc.scalar.activation(pa[:], a[:], ACT.Exp, scale=1.0 / SOFTEN, accum_out=soft_sum[:])
         neg_shift = held.tile([P, 1], F32, name="neg_shift")
-        nc.vector.tensor_scalar(
-            neg_shift[:], soft_sum[:].bitcast(I32), -SOFTEN * math.log(2.0) / 2**23, SOFTEN * math.log(2.0) * 127, ALU.mult, ALU.add
+        nc.scalar.activation(
+            neg_shift[:],
+            soft_sum[:].bitcast(U32),
+            ACT.Copy,
+            scale=-SOFTEN * math.log(2.0) / 2**23,
+            bias=SOFTEN * math.log(2.0) * 127,
         )
         g = quantize(grouped_g, "g")
         shifted = held.tile([P, I], F32, name="shifted", tag="shifted")
         nc.vector.tensor_tensor(by_page(shifted[:]), by_page(b[:]), over_page(page_max[:]), ALU.subtract)
 
-        z = held.tile([P, 1], F32, name="z")
-        nc.scalar.activation(pa[:], a[:], ACT.Exp, bias=neg_shift[:], accum_out=z[:])
+        sums = held.tile([P, G + 1], F32, name="sums")
+        sb, z = sums[:, :G], sums[:, G:]
+        nc.scalar.activation(pa[:], a[:], ACT.Exp, bias=neg_shift[:], accum_out=z)
         pb = held.tile([P, I], F32, name="pb")
         nc.scalar.activation(pb[:], shifted[:], ACT.Exp)
 
@@ -166,15 +172,13 @@ def tile_attend_bpagethensecond_s_kernel(
         half_sums = psum.tile([P, 2 * G], F32, name="half_sums")
         nc.tensor.transpose(half_sums[:], turned_sb[:], identity[:])
 
-        sb = held.tile([P, G], F32, name="sb")
-        nc.vector.tensor_reduce(sb[:], by_page(pb[:]), AX.X, ALU.add)
-        inv_z = held.tile([P, 1], F32, name="inv_z")
-        nc.vector.reciprocal(inv_z[:], z[:])
+        nc.vector.tensor_reduce(sb, by_page(pb[:]), AX.X, ALU.add)
 
         drr = held.tile([P, I], F32, name="drr")
         nc.vector.tensor_tensor(drr[:], c[:], pb[:], ALU.mult)
-        inv_sb = held.tile([P, G], F32, name="inv_sb", tag="val_plane", align_bytes=64)
-        nc.vector.reciprocal(inv_sb[:], sb[:])
+        inverses = held.tile([P, G + 1], F32, name="inverses", tag="val_plane", align_bytes=64)
+        nc.vector.reciprocal(inverses[:], sums[:])
+        inv_sb, inv_z = inverses[:, :G], inverses[:, G:]
         dr = held.tile([P, G], F32, name="dr")
         nc.vector.tensor_reduce(dr[:], by_page(drr[:]), AX.X, ALU.add)
 
@@ -185,10 +189,10 @@ def tile_attend_bpagethensecond_s_kernel(
             return ap.unsqueeze(2).to_broadcast([P, G, 2])
 
         share = held.tile([P, 2 * G], F32, name="share")
-        nc.vector.scalar_tensor_tensor(by_half(share[:]), by_half(half_sums[:]), inv_z[:], over_half(inv_sb[:]), ALU.mult, ALU.mult)
+        nc.vector.scalar_tensor_tensor(by_half(share[:]), by_half(half_sums[:]), inv_z, over_half(inv_sb), ALU.mult, ALU.mult)
 
         page_grad = held.tile([P, G], F32, name="page_grad")
-        nc.vector.scalar_tensor_tensor(page_grad[:], dr[:], GAIN, inv_sb[:], ALU.mult, ALU.mult)
+        nc.vector.scalar_tensor_tensor(page_grad[:], dr[:], GAIN, inv_sb, ALU.mult, ALU.mult)
         weighted = held.tile([P, 2 * G], F32, name="weighted")
         mean_grad = held.tile([P, 1], F32, name="mean_grad")
         nc.vector.scalar_tensor_tensor(
@@ -196,7 +200,7 @@ def tile_attend_bpagethensecond_s_kernel(
         )
 
         r1 = held.tile([P, I], F32, name="r1")
-        nc.vector.tensor_scalar(by_page(r1[:]), over_page(page_grad[:]), mean_grad[:], inv_z[:], ALU.subtract, ALU.mult)
+        nc.vector.tensor_scalar(by_page(r1[:]), over_page(page_grad[:]), mean_grad[:], inv_z, ALU.subtract, ALU.mult)
         nc.vector.tensor_tensor(window[:].indirect(offsets[:]), r1[:], pa[:], ALU.mult)
 
         start = 0

@@ -124,10 +124,6 @@ def tile_attend_bpagethensecond_s_kernel(
         q2 = quantize(grouped_q2, "q2")
         b = scores(q2, key_codes, key_plane, "b")
 
-        grouped_g = interleave(raw_g, "grouped_g")
-
-        before = held.tile([P, T], F32, name="before", tag="raw_grad", align_bytes=64)
-        nc.sync.dma_start(before[:], old)
         val_codes = held.tile([P, I], U16, name="val_codes", tag="raw_second", align_bytes=64)
         nc.vector.tensor_copy(val_codes[:], val_words[:].indirect(offsets[:]))
 
@@ -135,7 +131,8 @@ def tile_attend_bpagethensecond_s_kernel(
         nc.vector.tensor_reduce(page_max[:], by_page(b[:]), AX.X, ALU.max)
         pa = held.tile([P, I], F32, name="pa")
         soft_sum = held.tile([P, 1], F32, name="soft_sum", tag="val_plane", align_bytes=64)
-        nc.scalar.activation(pa[:], a[:], ACT.Exp, scale=1.0 / SOFTEN, accum_out=soft_sum[:])
+        softened = held.tile([P, I], F32, name="softened", tag="grouped_g", align_bytes=64)
+        nc.scalar.activation(softened[:], a[:], ACT.Exp, scale=1.0 / SOFTEN, accum_out=soft_sum[:])
         neg_shift = held.tile([P, 1], F32, name="neg_shift")
         nc.scalar.activation(
             neg_shift[:],
@@ -144,7 +141,9 @@ def tile_attend_bpagethensecond_s_kernel(
             scale=-SOFTEN * math.log(2.0) / 2**23,
             bias=SOFTEN * math.log(2.0) * 127,
         )
-        g = quantize(grouped_g, "g")
+        grouped_g = interleave(raw_g, "grouped_g")
+        before = held.tile([P, T], F32, name="before", tag="raw_grad", align_bytes=64)
+        nc.sync.dma_start(before[:], old)
         shifted = held.tile([P, I], F32, name="shifted", tag="shifted")
         nc.vector.tensor_tensor(by_page(shifted[:]), by_page(b[:]), over_page(page_max[:]), ALU.subtract)
 
@@ -154,6 +153,7 @@ def tile_attend_bpagethensecond_s_kernel(
         pb = held.tile([P, I], F32, name="pb")
         nc.scalar.activation(pb[:], shifted[:], ACT.Exp)
 
+        g = quantize(grouped_g, "g")
         val_plane = held.tile([P, I], U8, name="val_plane", tag="val_plane", align_bytes=64)
         for half in range(2):
             nc.vector.tensor_copy(

from contextlib import ExitStack

import math

import concourse.mybir as mybir
from concourse.masks import make_identity

D, T, I, Q, G = 512, 2048, 512, 128, 64
PAGE = I // G
P = 128
PACK = 4
GAIN = 512.0
FLOPS = 3 * 2 * D * Q * I

F32 = mybir.dt.float32
BF16 = mybir.dt.bfloat16
I32 = mybir.dt.int32
U32 = mybir.dt.uint32
U16 = mybir.dt.uint16
U8 = mybir.dt.uint8
FP8X4 = mybir.dt.float8_e4m3fn_x4
FP4X4 = mybir.dt.float4_e2m1fn_x4
ALU = mybir.AluOpType
ACT = mybir.ActivationFunctionType
AX = mybir.AxisListType

STORE_COLS = (256, 256, 512, 512, 256, 256)
SOFTEN = 8.0
QUARTER = 4
HALF = I // 2


def tile_attend_bpagethensecond_s_kernel(
    tc, query, query2, keys_words, keys_scales, gout, vals_words, vals_scales, old, offs, out
):
    nc = tc.nc
    with ExitStack() as ctx:
        held = ctx.enter_context(tc.tile_pool(name="held", bufs=1))
        psum = ctx.enter_context(tc.psum_pool(name="psum", bufs=1))

        offsets = held.tile([P, I // 16], U16, name="offsets")

        def load_words(words, name):
            tile = held.tile([P, T], U16, name=name, align_bytes=64)
            nc.sync.dma_start(tile[:].bitcast(I32), words[0].bitcast(I32))
            return tile

        def load_scales(scales, name):
            tile = held.tile([P, T], U8, name=name, tag=name, align_bytes=64)
            nc.vector.memset(tile[:].bitcast(I32), 0)
            for quad in range(4):
                nc.sync.dma_start(
                    tile[32 * quad : 32 * quad + 4, :].bitcast(I32),
                    scales[0, 4 * quad : 4 * quad + 4, :].bitcast(I32),
                )
            return tile

        def load_rows(x, tag, queue):
            raw = held.tile([P, PACK, Q], F32, name=tag, tag=tag, align_bytes=64)
            queue.dma_start(raw[:], x.rearrange("(p j) w -> p j w", j=PACK))
            return raw

        def interleave(raw, name):
            grouped = held.tile([P, Q, PACK], BF16, name=name, tag=name, align_bytes=64)
            nc.scalar.activation(grouped[:], raw[:].rearrange("p j w -> p w j"), ACT.Copy)
            return grouped

        def quantize(grouped, name):
            codes = held.tile([P, Q], U32, name=name + "_codes", tag=name, align_bytes=64)
            plane = held.tile([P, Q], U8, name=name + "_plane", align_bytes=64)
            nc.vector.quantize_mx(
                out=codes[:].bitcast(FP8X4),
                scales=plane[:],
                in_=grouped[:].rearrange("p w j -> p (w j)"),
            )
            return codes, plane

        def gather(table, dtype, name):
            picked = held.tile([P, I], dtype, name=name, align_bytes=64)
            nc.vector.tensor_copy(picked[:], table[:].indirect(offsets[:]))
            return picked

        def scores(quantized, words, plane, name, width=I):
            acc = psum.tile([P, I], F32, name=name)
            for first in range(0, I, width):
                slots = slice(first, first + width)
                nc.tensor.matmul_mx(
                    out=acc[:, slots],
                    lhsT=quantized[0][:].bitcast(FP8X4),
                    lhsT_scale=quantized[1][:],
                    rhs=words[:, slots].bitcast(FP4X4),
                    rhs_scale=plane[:, slots],
                    start=True,
                    stop=True,
                )
            return acc

        def by_page(ap):
            return ap.rearrange("p (g j) -> p g j", j=PAGE)

        def over_page(ap):
            return ap.unsqueeze(2).to_broadcast([P, G, PAGE])

        key_words = load_words(keys_words, "key_words")
        nc.sync.dma_start(offsets[:], offs)
        key_scales = load_scales(keys_scales, "key_scales")
        raw_q = load_rows(query, "raw_first", nc.sync)
        raw_q2 = load_rows(query2, "raw_second", nc.sync)
        val_words = load_words(vals_words, "val_words")
        raw_g = load_rows(gout, "raw_grad", nc.sync)
        val_scales = load_scales(vals_scales, "val_scales")
        window = held.tile([P, T], F32, name="window")
        nc.vector.memset(window[:], 0.0)
        identity = held.tile([P, P], F32, name="identity")
        nc.vector.memset(identity[:], 0.0)
        make_identity(nc, identity[:], nomemset=True)

        key_codes = gather(key_words, U16, "key_codes")
        key_plane = gather(key_scales, U8, "key_plane")
        grouped_q = interleave(raw_q, "grouped_q")
        grouped_q2 = interleave(raw_q2, "grouped_q2")
        q1 = quantize(grouped_q, "q1")
        a = scores(q1, key_codes, key_plane, "a")
        q2 = quantize(grouped_q2, "q2")
        b = scores(q2, key_codes, key_plane, "b")

        val_codes = held.tile([P, I], U16, name="val_codes", tag="raw_second", align_bytes=64)
        nc.vector.tensor_copy(val_codes[:], val_words[:].indirect(offsets[:]))

        page_max = held.tile([P, G], F32, name="page_max")
        nc.vector.tensor_reduce(page_max[:], by_page(b[:]), AX.X, ALU.max)
        pa = held.tile([P, I], F32, name="pa")
        soft_sum = held.tile([P, 1], F32, name="soft_sum", tag="val_plane", align_bytes=64)
        softened = held.tile([P, I], F32, name="softened", tag="grouped_g", align_bytes=64)
        nc.scalar.activation(softened[:], a[:], ACT.Exp, scale=1.0 / SOFTEN, accum_out=soft_sum[:])
        neg_shift = held.tile([P, 1], F32, name="neg_shift")
        nc.scalar.activation(
            neg_shift[:],
            soft_sum[:].bitcast(U32),
            ACT.Copy,
            scale=-SOFTEN * math.log(2.0) / 2**23,
            bias=SOFTEN * math.log(2.0) * 127,
        )
        grouped_g = interleave(raw_g, "grouped_g")
        before = held.tile([P, T], F32, name="before", tag="raw_grad", align_bytes=64)
        nc.sync.dma_start(before[:], old)
        shifted = held.tile([P, I], F32, name="shifted", tag="shifted")
        nc.vector.tensor_tensor(by_page(shifted[:]), by_page(b[:]), over_page(page_max[:]), ALU.subtract)

        sums = held.tile([P, G + 1], F32, name="sums")
        sb, z = sums[:, :G], sums[:, G:]
        nc.scalar.activation(pa[:], a[:], ACT.Exp, bias=neg_shift[:], accum_out=z)
        pb = held.tile([P, I], F32, name="pb")
        nc.scalar.activation(pb[:], shifted[:], ACT.Exp)

        g = quantize(grouped_g, "g")
        val_plane = held.tile([P, I], U8, name="val_plane", tag="val_plane", align_bytes=64)
        for half in range(2):
            nc.vector.tensor_copy(
                val_plane[:, half * HALF : (half + 1) * HALF],
                val_scales[:].indirect(offsets[:, half * HALF // 16 : (half + 1) * HALF // 16]),
            )

        turned = psum.tile([P, Q], F32, name="turned")
        for j in range(QUARTER):
            nc.tensor.matmul(
                turned[:], pa[:, j::QUARTER], identity[:], start=(j == 0), stop=(j == QUARTER - 1), is_transpose=True
            )
        c = scores(g, val_codes, val_plane, "c", HALF)
        turned_sb = held.tile([P, Q], F32, name="turned_sb")
        nc.scalar.copy(turned_sb[:], turned[:])
        half_sums = psum.tile([P, 2 * G], F32, name="half_sums")
        nc.tensor.transpose(half_sums[:], turned_sb[:], identity[:])

        nc.vector.tensor_reduce(sb, by_page(pb[:]), AX.X, ALU.add)

        drr = held.tile([P, I], F32, name="drr")
        nc.vector.tensor_tensor(drr[:], c[:], pb[:], ALU.mult)
        inverses = held.tile([P, G + 1], F32, name="inverses", tag="val_plane", align_bytes=64)
        nc.vector.reciprocal(inverses[:], sums[:])
        inv_sb, inv_z = inverses[:, :G], inverses[:, G:]
        dr = held.tile([P, G], F32, name="dr")
        nc.vector.tensor_reduce(dr[:], by_page(drr[:]), AX.X, ALU.add)

        def by_half(ap):
            return ap.rearrange("p (g h) -> p g h", h=2)

        def over_half(ap):
            return ap.unsqueeze(2).to_broadcast([P, G, 2])

        share = held.tile([P, 2 * G], F32, name="share")
        nc.vector.scalar_tensor_tensor(by_half(share[:]), by_half(half_sums[:]), inv_z, over_half(inv_sb), ALU.mult, ALU.mult)

        page_grad = held.tile([P, G], F32, name="page_grad")
        nc.vector.scalar_tensor_tensor(page_grad[:], dr[:], GAIN, inv_sb, ALU.mult, ALU.mult)
        weighted = held.tile([P, 2 * G], F32, name="weighted")
        mean_grad = held.tile([P, 1], F32, name="mean_grad")
        nc.vector.scalar_tensor_tensor(
            by_half(weighted[:]), over_half(dr[:]), GAIN, by_half(share[:]), ALU.mult, ALU.mult, accum_out=mean_grad[:]
        )

        r1 = held.tile([P, I], F32, name="r1")
        nc.vector.tensor_scalar(by_page(r1[:]), over_page(page_grad[:]), mean_grad[:], inv_z, ALU.subtract, ALU.mult)
        nc.vector.tensor_tensor(window[:].indirect(offsets[:]), r1[:], pa[:], ALU.mult)

        start = 0
        for n, width in enumerate(STORE_COLS):
            result = held.tile([P, width], F32, name="result%d" % n)
            nc.vector.tensor_tensor(result[:], window[:, start : start + width], before[:, start : start + width], ALU.add)
            queue = nc.sync if n % 2 == 0 else nc.scalar
            queue.dma_start(out[:, start : start + width], result[:])
            start = start + width
